import numpy as np
import ml_dtypes


def mxq(x, axis, fmt="e4m3"):
    dtype, down = {"e4m3": (ml_dtypes.float8_e4m3fn, 7), "e5m2": (ml_dtypes.float8_e5m2, 14)}[fmt]
    v = np.moveaxis(np.asarray(x, np.float32).astype(ml_dtypes.bfloat16).astype(np.float64), axis, -1)
    blocks = v.reshape(v.shape[:-1] + (-1, 32))
    amax = np.abs(blocks).max(-1, keepdims=True)
    byte = np.maximum(np.where(amax > 0, np.frexp(amax)[1] - 1 + 127, 0) - down, 1)
    scale = np.exp2(byte - 127.0)
    codes = (blocks / scale).astype(np.float32).astype(dtype).astype(np.float64)
    return np.moveaxis((codes * scale).reshape(v.shape), -1, axis)


WIDE = False


def mx_kscale(k):
    if not WIDE:
        return np.ones(k)
    levels = np.array([10, -10, 5, -5, 0])
    if k % 512:
        return np.exp2(np.random.permutation(np.resize(levels, k // 32))).repeat(32)
    a = np.empty((k // 512, 16))
    for p in range(k // 512):
        a[p, :8] = np.random.permutation(np.resize(levels, 8))
        for g in range(8):
            far = levels[np.abs(levels - a[p, g]) >= 10]
            a[p, g + 8] = far[np.random.randint(len(far))]
    return np.exp2(a.ravel()).repeat(32)


def f64(x):
    return np.asarray(x).astype(np.float64)


def striped(idx):
    return np.tile(idx.reshape(-1, 16).T, (8, 1)).astype(np.uint16)


def unstriped(offs):
    return offs[:16].T.reshape(-1).astype(np.int64)


def sigmoid(v):
    return 1.0 / (1.0 + np.exp(-np.maximum(v, -700.0)))


K, T, S, N, U = 512, 1024, 512, 256, 1024


def setup_inputs():
    n = np.random.standard_normal
    s = mx_kscale(K)[:, None]
    return {
        "xT": (n((K, T)) * s).astype(np.float32),
        "mem": n((N, U)).astype(np.float32),
        "w1": (n((K, N)) / np.sqrt(K) / s).astype(np.float32),
        "offs": striped(np.random.permutation(T)[:S]),
        "slot": striped(np.random.permutation(U)[:S]),
    }


def reference(xT, mem, w1, offs, slot):
    xq = mxq(f64(xT)[:, unstriped(offs)], 0, "e4m3")
    y = mxq(f64(w1), 0, "e4m3").T @ xq
    out = f64(mem).copy()
    out[:, unstriped(slot)] = f64(mem)[:, unstriped(slot)] * sigmoid(y)
    return out

@@ -1,0 +1,119 @@
+from contextlib import ExitStack
+
+import concourse.mybir as mybir
+
+K, T, S, N, U = 512, 1024, 512, 256, 1024
+FLOPS = 2 * K * N * S
+
+F32 = mybir.dt.float32
+BF16 = mybir.dt.bfloat16
+U32 = mybir.dt.uint32
+U16 = mybir.dt.uint16
+U8 = mybir.dt.uint8
+FP8X4 = mybir.dt.float8_e4m3fn_x4
+SIGMOID = mybir.ActivationFunctionType.Sigmoid
+MULT = mybir.AluOpType.mult
+
+P = 128
+PACK = 4
+HALVES = 2
+C = S // HALVES
+LC = C // 16
+BLOCKS = N // P
+
+
+def tile_picked_idxput_gate_e_kernel(tc, xT, mem, w1, offs, slot, out):
+    nc = tc.nc
+    with ExitStack() as ctx:
+        keep = ctx.enter_context(tc.tile_pool(name="keep", bufs=1))
+        psum = ctx.enter_context(tc.psum_pool(name="psum", bufs=1))
+
+        offs_sb = keep.tile([P, S // 16], U16, name="offs_sb")
+        slot_sb = keep.tile([P, S // 16], U16, name="slot_sb")
+        planes = [keep.tile([P, T], F32, name="plane%d" % j) for j in range(PACK)]
+        store = [keep.tile([P, U], F32, name="store%d" % b) for b in range(BLOCKS)]
+        w_raw = keep.tile([P, PACK, N], F32, name="w_raw")
+
+        warm_in = keep.tile([P, 1], F32, name="warm_in")
+        warm_out = keep.tile([P, 1], F32, name="warm_out")
+        nc.gpsimd.memset(warm_in[:], 0.0)
+        nc.scalar.activation(warm_out[:], warm_in[:], SIGMOID)
+
+        x_rows = xT.rearrange("(p j) t -> p j t", j=PACK)
+        nc.sync.dma_start(offs_sb[:], offs)
+        for j in range(PACK):
+            nc.sync.dma_start(planes[j][:], x_rows[:, j, :])
+        nc.sync.dma_start(slot_sb[:], slot)
+        nc.sync.dma_start(store[0][:], mem[0:P, :])
+        nc.sync.dma_start(w_raw[:], w1.rearrange("(p j) n -> p j n", j=PACK))
+        nc.sync.dma_start(store[1][:], mem[P : 2 * P, :])
+
+        picked = keep.tile([P, HALVES, PACK, C], BF16, name="picked", align_bytes=64)
+        for j in range(PACK - 1):
+            nc.vector.tensor_copy(picked[:, :, j, :], planes[j][:].indirect(offs_sb[:]))
+        for h in range(HALVES):
+            nc.vector.tensor_copy(
+                picked[:, h, PACK - 1, :], planes[PACK - 1][:].indirect(offs_sb[:, h * LC : (h + 1) * LC])
+            )
+
+        old = [keep.tile([P, S], F32, name="old%d" % b) for b in range(BLOCKS)]
+        x_codes, x_scales, w_codes, w_scales = [], [], [], []
+
+        def weave_x(h):
+            woven = keep.tile([P, C, PACK], BF16, name="x_woven%d" % h, align_bytes=64)
+            nc.scalar.copy(woven[:], picked[:, h].rearrange("p j c -> p c j"))
+            return woven
+
+        def weave_w(b):
+            woven = keep.tile([P, P, PACK], BF16, name="w_woven%d" % b, align_bytes=64)
+            nc.scalar.copy(woven[:], w_raw[:, :, b * P : (b + 1) * P].rearrange("p j c -> p c j"))
+            return woven
+
+        def quantize(woven, width, name):
+            codes = keep.tile([P, width], U32, name=name + "_codes", align_bytes=64)
+            scales = keep.tile([P, width], U8, name=name + "_scales", align_bytes=64)
+            nc.vector.quantize_mx(
+                out=codes[:].bitcast(FP8X4), scales=scales[:], in_=woven[:].rearrange("p c j -> p (c j)")
+            )
+            return codes, scales
+
+        def gate(b, h, xq, wq):
+            acc = psum.tile([P, C], F32, name="acc%d%d" % (b, h))
+            nc.tensor.matmul_mx(
+                out=acc[:],
+                lhsT=wq[0][:].bitcast(FP8X4),
+                lhsT_scale=wq[1][:],
+                rhs=xq[0][:].bitcast(FP8X4),
+                rhs_scale=xq[1][:],
+                start=True,
+                stop=True,
+            )
+            g = keep.tile([P, C], F32, name="gate%d%d" % (b, h))
+            nc.scalar.activation(g[:], acc[:], SIGMOID)
+            return g
+
+        def put(b, h, g):
+            nc.vector.tensor_tensor(
+                store[b][:].indirect(slot_sb[:, h * LC : (h + 1) * LC]), old[b][:, h * C : (h + 1) * C], g[:], MULT
+            )
+
+        xa = weave_x(0)
+        nc.vector.tensor_copy(old[0][:], store[0][:].indirect(slot_sb[:]))
+        xqa = quantize(xa, C, "xa")
+        w0 = weave_w(0)
+        w1w = weave_w(1)
+        wq0 = quantize(w0, P, "w0")
+        g00 = gate(0, 0, xqa, wq0)
+        nc.vector.tensor_copy(old[1][:], store[1][:].indirect(slot_sb[:]))
+        wq1 = quantize(w1w, P, "w1")
+        g10 = gate(1, 0, xqa, wq1)
+        xb = weave_x(1)
+        put(0, 0, g00)
+        xqb = quantize(xb, C, "xb")
+        g01 = gate(0, 1, xqb, wq0)
+        g11 = gate(1, 1, xqb, wq1)
+        put(1, 0, g10)
+        put(0, 1, g01)
+        nc.sync.dma_start(out[0:P, :], store[0][:])
+        put(1, 1, g11)
+        nc.sync.dma_start(out[P : 2 * P, :], store[1][:])

@@ -41,31 +41,32 @@ def tile_picked_idxput_gate_e_kernel(tc, xT, mem, w1, offs, slot, out):
 
         x_rows = xT.rearrange("(p j) t -> p j t", j=PACK)
         nc.sync.dma_start(offs_sb[:], offs)
-        for j in range(PACK):
-            nc.sync.dma_start(planes[j][:], x_rows[:, j, :])
+        nc.sync.dma_start(planes[0][:], x_rows[:, 0, :])
         nc.sync.dma_start(slot_sb[:], slot)
+        for j in range(1, PACK):
+            nc.sync.dma_start(planes[j][:], x_rows[:, j, :])
         nc.sync.dma_start(store[0][:], mem[0:P, :])
         nc.sync.dma_start(w_raw[:], w1.rearrange("(p j) n -> p j n", j=PACK))
         nc.sync.dma_start(store[1][:], mem[P : 2 * P, :])
 
-        picked = keep.tile([P, HALVES, PACK, C], BF16, name="picked", align_bytes=64)
+        picked = keep.tile([P, PACK, S], BF16, name="picked", align_bytes=64)
         for j in range(PACK - 1):
-            nc.vector.tensor_copy(picked[:, :, j, :], planes[j][:].indirect(offs_sb[:]))
+            nc.vector.tensor_copy(picked[:, j, :], planes[j][:].indirect(offs_sb[:]))
         for h in range(HALVES):
             nc.vector.tensor_copy(
-                picked[:, h, PACK - 1, :], planes[PACK - 1][:].indirect(offs_sb[:, h * LC : (h + 1) * LC])
+                picked[:, PACK - 1, h * C : (h + 1) * C], planes[PACK - 1][:].indirect(offs_sb[:, h * LC : (h + 1) * LC])
             )
 
         old = [keep.tile([P, S], F32, name="old%d" % b) for b in range(BLOCKS)]
         x_codes, x_scales, w_codes, w_scales = [], [], [], []
 
         def weave_x(h):
-            woven = keep.tile([P, C, PACK], BF16, name="x_woven%d" % h, align_bytes=64)
-            nc.scalar.copy(woven[:], picked[:, h].rearrange("p j c -> p c j"))
+            woven = keep.tile([P, C, PACK], BF16, name="x_woven%d" % h, tag="woven_x" if h == 0 else "woven_late", align_bytes=64)
+            nc.scalar.copy(woven[:], picked[:, :, h * C : (h + 1) * C].rearrange("p j c -> p c j"))
             return woven
 
         def weave_w(b):
-            woven = keep.tile([P, P, PACK], BF16, name="w_woven%d" % b, align_bytes=64)
+            woven = keep.tile([P, P, PACK], BF16, name="w_woven%d" % b, tag="woven_w" if b == 0 else "woven_late", align_bytes=64)
             nc.scalar.copy(woven[:], w_raw[:, :, b * P : (b + 1) * P].rearrange("p j c -> p c j"))
             return woven
 
@@ -107,8 +108,8 @@ def tile_picked_idxput_gate_e_kernel(tc, xT, mem, w1, offs, slot, out):
         nc.vector.tensor_copy(old[1][:], store[1][:].indirect(slot_sb[:]))
         wq1 = quantize(w1w, P, "w1")
         g10 = gate(1, 0, xqa, wq1)
-        xb = weave_x(1)
         put(0, 0, g00)
+        xb = weave_x(1)
         xqb = quantize(xb, C, "xb")
         g01 = gate(0, 1, xqb, wq0)
         g11 = gate(1, 1, xqb, wq1)

@@ -12,6 +12,7 @@ U16 = mybir.dt.uint16
 U8 = mybir.dt.uint8
 FP8X4 = mybir.dt.float8_e4m3fn_x4
 SIGMOID = mybir.ActivationFunctionType.Sigmoid
+COPY = mybir.ActivationFunctionType.Copy
 MULT = mybir.AluOpType.mult
 
 P = 128
@@ -32,7 +33,11 @@ def tile_picked_idxput_gate_e_kernel(tc, xT, mem, w1, offs, slot, out):
         slot_sb = keep.tile([P, S // 16], U16, name="slot_sb")
         planes = [keep.tile([P, T], F32, name="plane%d" % j) for j in range(PACK)]
         store = [keep.tile([P, U], F32, name="store%d" % b) for b in range(BLOCKS)]
-        w_raw = keep.tile([P, PACK, N], F32, name="w_raw")
+        shared = ctx.enter_context(tc.tile_pool(name="shared", bufs=1))
+        w_raw = [
+            shared.tile([P, PACK, P], F32, name="w_raw0", offset=1024, align_bytes=64),
+            keep.tile([P, PACK, P], F32, name="w_raw1", tag="w_raw1"),
+        ]
 
         warm_in = keep.tile([P, 1], F32, name="warm_in")
         warm_out = keep.tile([P, 1], F32, name="warm_out")
@@ -40,46 +45,53 @@ def tile_picked_idxput_gate_e_kernel(tc, xT, mem, w1, offs, slot, out):
         nc.scalar.activation(warm_out[:], warm_in[:], SIGMOID)
 
         x_rows = xT.rearrange("(p j) t -> p j t", j=PACK)
+        w_rows = w1.rearrange("(p j) n -> p j n", j=PACK)
         nc.sync.dma_start(offs_sb[:], offs)
         nc.sync.dma_start(planes[0][:], x_rows[:, 0, :])
         nc.sync.dma_start(slot_sb[:], slot)
         for j in range(1, PACK):
             nc.sync.dma_start(planes[j][:], x_rows[:, j, :])
-        nc.sync.dma_start(store[0][:], mem[0:P, :])
-        nc.sync.dma_start(w_raw[:], w1.rearrange("(p j) n -> p j n", j=PACK))
-        nc.sync.dma_start(store[1][:], mem[P : 2 * P, :])
+        for b in range(BLOCKS):
+            nc.sync.dma_start(store[b][:], mem[b * P : (b + 1) * P, :])
+            nc.sync.dma_start(w_raw[b][:], w_rows[:, :, b * P : (b + 1) * P])
+
+        first, second = slice(0, C), slice(C, S)
+
+        def part(lst, cols):
+            return lst[:, cols.start // 16 : cols.stop // 16]
 
         picked = keep.tile([P, PACK, S], BF16, name="picked", align_bytes=64)
-        for j in range(PACK - 1):
-            nc.vector.tensor_copy(picked[:, j, :], planes[j][:].indirect(offs_sb[:]))
-        for h in range(HALVES):
-            nc.vector.tensor_copy(
-                picked[:, PACK - 1, h * C : (h + 1) * C], planes[PACK - 1][:].indirect(offs_sb[:, h * LC : (h + 1) * LC])
-            )
+        woven_a = keep.tile([P, C, PACK], BF16, name="woven_a", align_bytes=64)
+        rounded = keep.tile([P, T], BF16, name="rounded", align_bytes=64)
+        nc.vector.tensor_copy(picked[:, 0, :], planes[0][:].indirect(offs_sb[:]))
+        nc.vector.tensor_copy(picked[:, 1, first], planes[1][:].indirect(part(offs_sb, first)))
+        nc.scalar.copy(rounded[:], planes[1][:])
+        nc.scalar.activation(picked[:, 1, second], rounded[:].indirect(part(offs_sb, second)), COPY)
+        nc.vector.tensor_copy(picked[:, 2, :], planes[2][:].indirect(offs_sb[:]))
+        nc.vector.tensor_copy(picked[:, 3, first], planes[3][:].indirect(part(offs_sb, first)))
+        nc.scalar.copy(woven_a[:], picked[:, :, first].rearrange("p j c -> p c j"))
+        nc.vector.tensor_copy(picked[:, 3, second], planes[3][:].indirect(part(offs_sb, second)))
 
-        old = [keep.tile([P, S], F32, name="old%d" % b) for b in range(BLOCKS)]
-        x_codes, x_scales, w_codes, w_scales = [], [], [], []
+        old = [keep.tile([P, S], F32, name="old0"), shared.tile([P, S], F32, name="old1", offset=2048, align_bytes=64)]
 
-        def weave_x(h):
-            woven = keep.tile([P, C, PACK], BF16, name="x_woven%d" % h, tag="woven_x" if h == 0 else "woven_late", align_bytes=64)
-            nc.scalar.copy(woven[:], picked[:, :, h * C : (h + 1) * C].rearrange("p j c -> p c j"))
-            return woven
+        def look_up(b):
+            nc.vector.tensor_copy(old[b][:], store[b][:].indirect(slot_sb[:]))
 
         def weave_w(b):
-            woven = keep.tile([P, P, PACK], BF16, name="w_woven%d" % b, tag="woven_w" if b == 0 else "woven_late", align_bytes=64)
-            nc.scalar.copy(woven[:], w_raw[:, :, b * P : (b + 1) * P].rearrange("p j c -> p c j"))
-            return woven
+            tile = keep.tile([P, P, PACK], BF16, name="w_woven%d" % b, align_bytes=64)
+            nc.scalar.copy(tile[:], w_raw[b][:].rearrange("p j c -> p c j"))
+            return tile
 
-        def quantize(woven, width, name):
+        def quantize(tile, width, name):
             codes = keep.tile([P, width], U32, name=name + "_codes", align_bytes=64)
             scales = keep.tile([P, width], U8, name=name + "_scales", align_bytes=64)
             nc.vector.quantize_mx(
-                out=codes[:].bitcast(FP8X4), scales=scales[:], in_=woven[:].rearrange("p c j -> p (c j)")
+                out=codes[:].bitcast(FP8X4), scales=scales[:], in_=tile[:].rearrange("p c j -> p (c j)")
             )
             return codes, scales
 
-        def gate(b, h, xq, wq):
-            acc = psum.tile([P, C], F32, name="acc%d%d" % (b, h))
+        def gate(name, xq, wq, dst):
+            acc = psum.tile([P, C], F32, name="acc" + name)
             nc.tensor.matmul_mx(
                 out=acc[:],
                 lhsT=wq[0][:].bitcast(FP8X4),
@@ -89,32 +101,28 @@ def tile_picked_idxput_gate_e_kernel(tc, xT, mem, w1, offs, slot, out):
                 start=True,
                 stop=True,
             )
-            g = keep.tile([P, C], F32, name="gate%d%d" % (b, h))
-            nc.scalar.activation(g[:], acc[:], SIGMOID)
-            return g
+            nc.scalar.activation(dst, acc[:], SIGMOID)
 
-        def put(b, h, g):
-            nc.vector.tensor_tensor(
-                store[b][:].indirect(slot_sb[:, h * LC : (h + 1) * LC]), old[b][:, h * C : (h + 1) * C], g[:], MULT
-            )
+        def put(b, cols, g):
+            nc.vector.tensor_tensor(store[b][:].indirect(part(slot_sb, cols)), old[b][:, cols], g, MULT)
 
-        xa = weave_x(0)
-        nc.vector.tensor_copy(old[0][:], store[0][:].indirect(slot_sb[:]))
-        xqa = quantize(xa, C, "xa")
-        w0 = weave_w(0)
-        w1w = weave_w(1)
-        wq0 = quantize(w0, P, "w0")
-        g00 = gate(0, 0, xqa, wq0)
-        nc.vector.tensor_copy(old[1][:], store[1][:].indirect(slot_sb[:]))
-        wq1 = quantize(w1w, P, "w1")
-        g10 = gate(1, 0, xqa, wq1)
-        put(0, 0, g00)
-        xb = weave_x(1)
-        xqb = quantize(xb, C, "xb")
-        g01 = gate(0, 1, xqb, wq0)
-        g11 = gate(1, 1, xqb, wq1)
-        put(1, 0, g10)
-        put(0, 1, g01)
+        look_up(0)
+        xqa = quantize(woven_a, C, "xa")
+        wq0 = quantize(weave_w(0), P, "w0")
+        look_up(1)
+        woven_b = shared.tile([P, C, PACK], BF16, name="woven_b", offset=0, align_bytes=64)
+        nc.scalar.copy(woven_b[:], picked[:, :, second].rearrange("p j c -> p c j"))
+        xqb = quantize(woven_b, C, "xb")
+        g0a = keep.tile([P, C], F32, name="gate0a")
+        gate("0a", xqa, wq0, g0a[:])
+        put(0, first, g0a[:])
+        wq1 = quantize(weave_w(1), P, "w1")
+        g0b = keep.tile([P, C], F32, name="gate0b", tag="w_raw1")
+        gate("0b", xqb, wq0, g0b[:])
+        g1 = keep.tile([P, S], F32, name="gate1")
+        gate("1a", xqa, wq1, g1[:, first])
+        gate("1b", xqb, wq1, g1[:, second])
+        put(0, second, g0b[:])
         nc.sync.dma_start(out[0:P, :], store[0][:])
-        put(1, 1, g11)
+        put(1, slice(0, S), g1[:])
         nc.sync.dma_start(out[P : 2 * P, :], store[1][:])

@@ -33,11 +33,7 @@ def tile_picked_idxput_gate_e_kernel(tc, xT, mem, w1, offs, slot, out):
         slot_sb = keep.tile([P, S // 16], U16, name="slot_sb")
         planes = [keep.tile([P, T], F32, name="plane%d" % j) for j in range(PACK)]
         store = [keep.tile([P, U], F32, name="store%d" % b) for b in range(BLOCKS)]
-        shared = ctx.enter_context(tc.tile_pool(name="shared", bufs=1))
-        w_raw = [
-            shared.tile([P, PACK, P], F32, name="w_raw0", offset=1024, align_bytes=64),
-            keep.tile([P, PACK, P], F32, name="w_raw1", tag="w_raw1"),
-        ]
+        w_raw = [keep.tile([P, PACK, P], F32, name="w_raw%d" % b, tag="w_raw%d" % b, align_bytes=64) for b in range(BLOCKS)]
 
         warm_in = keep.tile([P, 1], F32, name="warm_in")
         warm_out = keep.tile([P, 1], F32, name="warm_out")
@@ -48,31 +44,33 @@ def tile_picked_idxput_gate_e_kernel(tc, xT, mem, w1, offs, slot, out):
         w_rows = w1.rearrange("(p j) n -> p j n", j=PACK)
         nc.sync.dma_start(offs_sb[:], offs)
         nc.sync.dma_start(planes[0][:], x_rows[:, 0, :])
-        nc.sync.dma_start(slot_sb[:], slot)
         for j in range(1, PACK):
             nc.sync.dma_start(planes[j][:], x_rows[:, j, :])
+        nc.sync.dma_start(w_raw[0][:], w_rows[:, :, 0:P])
+        nc.sync.dma_start(slot_sb[:], slot)
+        table0 = keep.tile([P, U], F32, name="table0")
+        nc.sync.dma_start(table0[:], mem[0:P, :])
         for b in range(BLOCKS):
             nc.sync.dma_start(store[b][:], mem[b * P : (b + 1) * P, :])
-            nc.sync.dma_start(w_raw[b][:], w_rows[:, :, b * P : (b + 1) * P])
+        nc.sync.dma_start(w_raw[1][:], w_rows[:, :, P : 2 * P])
 
         first, second = slice(0, C), slice(C, S)
 
         def part(lst, cols):
             return lst[:, cols.start // 16 : cols.stop // 16]
 
-        picked = keep.tile([P, PACK, S], BF16, name="picked", align_bytes=64)
         woven_a = keep.tile([P, C, PACK], BF16, name="woven_a", align_bytes=64)
-        rounded = keep.tile([P, T], BF16, name="rounded", align_bytes=64)
-        nc.vector.tensor_copy(picked[:, 0, :], planes[0][:].indirect(offs_sb[:]))
-        nc.vector.tensor_copy(picked[:, 1, first], planes[1][:].indirect(part(offs_sb, first)))
-        nc.scalar.copy(rounded[:], planes[1][:])
-        nc.scalar.activation(picked[:, 1, second], rounded[:].indirect(part(offs_sb, second)), COPY)
-        nc.vector.tensor_copy(picked[:, 2, :], planes[2][:].indirect(offs_sb[:]))
-        nc.vector.tensor_copy(picked[:, 3, first], planes[3][:].indirect(part(offs_sb, first)))
-        nc.scalar.copy(woven_a[:], picked[:, :, first].rearrange("p j c -> p c j"))
-        nc.vector.tensor_copy(picked[:, 3, second], planes[3][:].indirect(part(offs_sb, second)))
+        picked_b = keep.tile([P, PACK, C], BF16, name="picked_b", align_bytes=64)
+        for j in range(PACK):
+            nc.vector.tensor_copy(woven_a[:, :, j], planes[j][:].indirect(part(offs_sb, first)))
+            if j < 2:
+                rounded = keep.tile([P, T], BF16, name="rounded%d" % j, align_bytes=64)
+                nc.scalar.copy(rounded[:], planes[j][:])
+                nc.scalar.activation(picked_b[:, j, :], rounded[:].indirect(part(offs_sb, second)), COPY)
+            else:
+                nc.vector.tensor_copy(picked_b[:, j, :], planes[j][:].indirect(part(offs_sb, second)))
 
-        old = [keep.tile([P, S], F32, name="old0"), shared.tile([P, S], F32, name="old1", offset=2048, align_bytes=64)]
+        old = [keep.tile([P, S], F32, name="old%d" % b) for b in range(BLOCKS)]
 
         def look_up(b):
             nc.vector.tensor_copy(old[b][:], store[b][:].indirect(slot_sb[:]))
@@ -106,18 +104,19 @@ def tile_picked_idxput_gate_e_kernel(tc, xT, mem, w1, offs, slot, out):
         def put(b, cols, g):
             nc.vector.tensor_tensor(store[b][:].indirect(part(slot_sb, cols)), old[b][:, cols], g, MULT)
 
-        look_up(0)
         xqa = quantize(woven_a, C, "xa")
         wq0 = quantize(weave_w(0), P, "w0")
-        look_up(1)
-        woven_b = shared.tile([P, C, PACK], BF16, name="woven_b", offset=0, align_bytes=64)
-        nc.scalar.copy(woven_b[:], picked[:, :, second].rearrange("p j c -> p c j"))
+        for cols in (first, second):
+            nc.vector.tensor_copy(old[0][:, cols], table0[:].indirect(part(slot_sb, cols)))
+        woven_b = keep.tile([P, C, PACK], BF16, name="woven_b", tag="w_raw0", align_bytes=64)
+        nc.scalar.copy(woven_b[:], picked_b[:].rearrange("p j c -> p c j"))
         xqb = quantize(woven_b, C, "xb")
         g0a = keep.tile([P, C], F32, name="gate0a")
         gate("0a", xqa, wq0, g0a[:])
         put(0, first, g0a[:])
+        look_up(1)
         wq1 = quantize(weave_w(1), P, "w1")
-        g0b = keep.tile([P, C], F32, name="gate0b", tag="w_raw1")
+        g0b = keep.tile([P, C], F32, name="gate0b", tag="w_raw1", align_bytes=64)
         gate("0b", xqb, wq0, g0b[:])
         g1 = keep.tile([P, S], F32, name="gate1")
         gate("1a", xqa, wq1, g1[:, first])

@@ -43,8 +43,7 @@ def tile_picked_idxput_gate_e_kernel(tc, xT, mem, w1, offs, slot, out):
         x_rows = xT.rearrange("(p j) t -> p j t", j=PACK)
         w_rows = w1.rearrange("(p j) n -> p j n", j=PACK)
         nc.sync.dma_start(offs_sb[:], offs)
-        nc.sync.dma_start(planes[0][:], x_rows[:, 0, :])
-        for j in range(1, PACK):
+        for j in (2, 0, 1, 3):
             nc.sync.dma_start(planes[j][:], x_rows[:, j, :])
         nc.sync.dma_start(w_raw[0][:], w_rows[:, :, 0:P])
         nc.sync.dma_start(slot_sb[:], slot)
@@ -60,15 +59,23 @@ def tile_picked_idxput_gate_e_kernel(tc, xT, mem, w1, offs, slot, out):
             return lst[:, cols.start // 16 : cols.stop // 16]
 
         woven_a = keep.tile([P, C, PACK], BF16, name="woven_a", align_bytes=64)
+        picked_a = keep.tile([P, 2, C], BF16, name="picked_a", align_bytes=64)
         picked_b = keep.tile([P, PACK, C], BF16, name="picked_b", align_bytes=64)
-        for j in range(PACK):
-            nc.vector.tensor_copy(woven_a[:, :, j], planes[j][:].indirect(part(offs_sb, first)))
-            if j < 2:
-                rounded = keep.tile([P, T], BF16, name="rounded%d" % j, align_bytes=64)
-                nc.scalar.copy(rounded[:], planes[j][:])
-                nc.scalar.activation(picked_b[:, j, :], rounded[:].indirect(part(offs_sb, second)), COPY)
-            else:
-                nc.vector.tensor_copy(picked_b[:, j, :], planes[j][:].indirect(part(offs_sb, second)))
+        rounded = keep.tile([P, T], BF16, name="rounded", align_bytes=64)
+
+        def pick(dst, j, cols):
+            nc.vector.tensor_copy(dst, planes[j][:].indirect(part(offs_sb, cols)))
+
+        pick(woven_a[:, :, 2], 2, first)
+        pick(picked_b[:, 2, :], 2, second)
+        pick(picked_a[:, 0, :], 0, first)
+        nc.scalar.copy(rounded[:], planes[0][:])
+        nc.scalar.activation(picked_b[:, 0, :], rounded[:].indirect(part(offs_sb, second)), COPY)
+        pick(picked_a[:, 1, :], 1, first)
+        nc.scalar.copy(woven_a[:, :, 0:2], picked_a[:].rearrange("p j c -> p c j"))
+        pick(picked_b[:, 1, :], 1, second)
+        pick(woven_a[:, :, 3], 3, first)
+        pick(picked_b[:, 3, :], 3, second)
 
         old = [keep.tile([P, S], F32, name="old%d" % b) for b in range(BLOCKS)]
 

@@ -47,11 +47,9 @@ def tile_picked_idxput_gate_e_kernel(tc, xT, mem, w1, offs, slot, out):
             nc.sync.dma_start(planes[j][:], x_rows[:, j, :])
         nc.sync.dma_start(w_raw[0][:], w_rows[:, :, 0:P])
         nc.sync.dma_start(slot_sb[:], slot)
-        table0 = keep.tile([P, U], F32, name="table0")
-        nc.sync.dma_start(table0[:], mem[0:P, :])
-        for b in range(BLOCKS):
-            nc.sync.dma_start(store[b][:], mem[b * P : (b + 1) * P, :])
+        nc.sync.dma_start(store[0][:], mem[0:P, :])
         nc.sync.dma_start(w_raw[1][:], w_rows[:, :, P : 2 * P])
+        nc.sync.dma_start(store[1][:], mem[P : 2 * P, :])
 
         first, second = slice(0, C), slice(C, S)
 
@@ -113,8 +111,7 @@ def tile_picked_idxput_gate_e_kernel(tc, xT, mem, w1, offs, slot, out):
 
         xqa = quantize(woven_a, C, "xa")
         wq0 = quantize(weave_w(0), P, "w0")
-        for cols in (first, second):
-            nc.vector.tensor_copy(old[0][:, cols], table0[:].indirect(part(slot_sb, cols)))
+        look_up(0)
         woven_b = keep.tile([P, C, PACK], BF16, name="woven_b", tag="w_raw0", align_bytes=64)
         nc.scalar.copy(woven_b[:], picked_b[:].rearrange("p j c -> p c j"))
         xqb = quantize(woven_b, C, "xb")

@@ -17,10 +17,10 @@ MULT = mybir.AluOpType.mult
 
 P = 128
 PACK = 4
-HALVES = 2
-C = S // HALVES
-LC = C // 16
+HALF = S // 2
 BLOCKS = N // P
+PER_COLUMN = 16
+RUN = 4
 
 
 def tile_picked_idxput_gate_e_kernel(tc, xT, mem, w1, offs, slot, out):
@@ -29,103 +29,111 @@ def tile_picked_idxput_gate_e_kernel(tc, xT, mem, w1, offs, slot, out):
         keep = ctx.enter_context(tc.tile_pool(name="keep", bufs=1))
         psum = ctx.enter_context(tc.psum_pool(name="psum", bufs=1))
 
-        offs_sb = keep.tile([P, S // 16], U16, name="offs_sb")
-        slot_sb = keep.tile([P, S // 16], U16, name="slot_sb")
-        planes = [keep.tile([P, T], F32, name="plane%d" % j) for j in range(PACK)]
+        offs_sb = keep.tile([P, S // PER_COLUMN], U16, name="offs_sb")
+        slot_sb = keep.tile([P, S // PER_COLUMN], U16, name="slot_sb")
+        planes = [keep.tile([P, T], F32, name="plane%d" % t) for t in range(PACK)]
         store = [keep.tile([P, U], F32, name="store%d" % b) for b in range(BLOCKS)]
-        w_raw = [keep.tile([P, PACK, P], F32, name="w_raw%d" % b, tag="w_raw%d" % b, align_bytes=64) for b in range(BLOCKS)]
+        w_raw = [
+            keep.tile([P, PACK, P], F32, name="w_raw%d" % b, tag="w_raw%d" % b, align_bytes=64) for b in range(BLOCKS)
+        ]
 
         warm_in = keep.tile([P, 1], F32, name="warm_in")
         warm_out = keep.tile([P, 1], F32, name="warm_out")
-        nc.gpsimd.memset(warm_in[:], 0.0)
+        nc.vector.memset(warm_in[:], 0.0)
         nc.scalar.activation(warm_out[:], warm_in[:], SIGMOID)
 
-        x_rows = xT.rearrange("(p j) t -> p j t", j=PACK)
-        w_rows = w1.rearrange("(p j) n -> p j n", j=PACK)
+        x_rows = xT.rearrange("(p t) c -> p t c", t=PACK)
+        w_rows = w1.rearrange("(p t) n -> p t n", t=PACK)
+        nc.sync.dma_start(planes[2][:], x_rows[:, 2, :])
         nc.sync.dma_start(offs_sb[:], offs)
-        for j in (2, 0, 1, 3):
-            nc.sync.dma_start(planes[j][:], x_rows[:, j, :])
+        for t in (0, 1, 3):
+            nc.sync.dma_start(planes[t][:], x_rows[:, t, :])
         nc.sync.dma_start(w_raw[0][:], w_rows[:, :, 0:P])
         nc.sync.dma_start(slot_sb[:], slot)
         nc.sync.dma_start(store[0][:], mem[0:P, :])
         nc.sync.dma_start(w_raw[1][:], w_rows[:, :, P : 2 * P])
         nc.sync.dma_start(store[1][:], mem[P : 2 * P, :])
 
-        first, second = slice(0, C), slice(C, S)
+        first, second, whole = slice(0, HALF), slice(HALF, S), slice(0, S)
 
-        def part(lst, cols):
-            return lst[:, cols.start // 16 : cols.stop // 16]
+        def entries(list_sb, cols):
+            return list_sb[:, cols.start // PER_COLUMN : cols.stop // PER_COLUMN]
 
-        woven_a = keep.tile([P, C, PACK], BF16, name="woven_a", align_bytes=64)
-        picked_a = keep.tile([P, 2, C], BF16, name="picked_a", align_bytes=64)
-        picked_b = keep.tile([P, PACK, C], BF16, name="picked_b", align_bytes=64)
+        def pick(dst, t, cols):
+            nc.vector.tensor_copy(dst, planes[t][:].indirect(entries(offs_sb, cols)))
+
+        def weave(dst, src):
+            nc.scalar.copy(
+                dst[:].rearrange("p (c i) t -> p c t i", i=RUN), src[:].rearrange("p t (c i) -> p c t i", i=RUN)
+            )
+
+        woven_first = keep.tile([P, HALF, PACK], BF16, name="woven_first", align_bytes=64)
+        picked_first = keep.tile([P, 2, HALF], BF16, name="picked_first", align_bytes=64)
+        picked_second = keep.tile([P, PACK, HALF], BF16, name="picked_second", align_bytes=64)
         rounded = keep.tile([P, T], BF16, name="rounded", align_bytes=64)
-
-        def pick(dst, j, cols):
-            nc.vector.tensor_copy(dst, planes[j][:].indirect(part(offs_sb, cols)))
-
-        pick(woven_a[:, :, 2], 2, first)
-        pick(picked_b[:, 2, :], 2, second)
-        pick(picked_a[:, 0, :], 0, first)
+        pick(woven_first[:, :, 2], 2, first)
+        pick(picked_second[:, 2, :], 2, second)
+        pick(picked_first[:, 0, :], 0, first)
         nc.scalar.copy(rounded[:], planes[0][:])
-        nc.scalar.activation(picked_b[:, 0, :], rounded[:].indirect(part(offs_sb, second)), COPY)
-        pick(picked_a[:, 1, :], 1, first)
-        nc.scalar.copy(woven_a[:, :, 0:2], picked_a[:].rearrange("p j c -> p c j"))
-        pick(picked_b[:, 1, :], 1, second)
-        pick(woven_a[:, :, 3], 3, first)
-        pick(picked_b[:, 3, :], 3, second)
+        nc.scalar.activation(picked_second[:, 0, :], rounded[:].indirect(entries(offs_sb, second)), COPY)
+        pick(picked_first[:, 1, :], 1, first)
+        nc.scalar.copy(woven_first[:, :, 0:2], picked_first[:].rearrange("p t c -> p c t"))
+        pick(picked_second[:, 1, :], 1, second)
+        pick(woven_first[:, :, 3], 3, first)
+        pick(picked_second[:, 3, :], 3, second)
 
         old = [keep.tile([P, S], F32, name="old%d" % b) for b in range(BLOCKS)]
 
         def look_up(b):
             nc.vector.tensor_copy(old[b][:], store[b][:].indirect(slot_sb[:]))
 
-        def weave_w(b):
-            tile = keep.tile([P, P, PACK], BF16, name="w_woven%d" % b, align_bytes=64)
-            nc.scalar.copy(tile[:], w_raw[b][:].rearrange("p j c -> p c j"))
-            return tile
-
-        def quantize(tile, width, name):
+        def quantize(woven, width, name):
             codes = keep.tile([P, width], U32, name=name + "_codes", align_bytes=64)
             scales = keep.tile([P, width], U8, name=name + "_scales", align_bytes=64)
             nc.vector.quantize_mx(
-                out=codes[:].bitcast(FP8X4), scales=scales[:], in_=tile[:].rearrange("p c j -> p (c j)")
+                out=codes[:].bitcast(FP8X4), scales=scales[:], in_=woven[:].rearrange("p c t -> p (c t)")
             )
             return codes, scales
 
-        def gate(name, xq, wq, dst):
-            acc = psum.tile([P, C], F32, name="acc" + name)
+        def quantize_weights(b):
+            woven = keep.tile([P, P, PACK], BF16, name="w_woven%d" % b, align_bytes=64)
+            weave(woven, w_raw[b])
+            return quantize(woven, P, "w%d" % b)
+
+        def gate(dst, w_mx, x_mx, name):
+            acc = psum.tile([P, HALF], F32, name="acc_" + name)
             nc.tensor.matmul_mx(
                 out=acc[:],
-                lhsT=wq[0][:].bitcast(FP8X4),
-                lhsT_scale=wq[1][:],
-                rhs=xq[0][:].bitcast(FP8X4),
-                rhs_scale=xq[1][:],
+                lhsT=w_mx[0][:].bitcast(FP8X4),
+                lhsT_scale=w_mx[1][:],
+                rhs=x_mx[0][:].bitcast(FP8X4),
+                rhs_scale=x_mx[1][:],
                 start=True,
                 stop=True,
             )
             nc.scalar.activation(dst, acc[:], SIGMOID)
 
-        def put(b, cols, g):
-            nc.vector.tensor_tensor(store[b][:].indirect(part(slot_sb, cols)), old[b][:, cols], g, MULT)
+        def put(b, cols, gates):
+            nc.vector.tensor_tensor(store[b][:].indirect(entries(slot_sb, cols)), old[b][:, cols], gates, MULT)
 
-        xqa = quantize(woven_a, C, "xa")
-        wq0 = quantize(weave_w(0), P, "w0")
+        x_first = quantize(woven_first, HALF, "x_first")
+        w_block0 = quantize_weights(0)
         look_up(0)
-        woven_b = keep.tile([P, C, PACK], BF16, name="woven_b", tag="w_raw0", align_bytes=64)
-        nc.scalar.copy(woven_b[:], picked_b[:].rearrange("p j c -> p c j"))
-        xqb = quantize(woven_b, C, "xb")
-        g0a = keep.tile([P, C], F32, name="gate0a")
-        gate("0a", xqa, wq0, g0a[:])
-        put(0, first, g0a[:])
+        woven_second = keep.tile([P, HALF, PACK], BF16, name="woven_second", tag="w_raw0", align_bytes=64)
+        weave(woven_second, picked_second)
+        x_second = quantize(woven_second, HALF, "x_second")
+        gate0_first = keep.tile([P, HALF], F32, name="gate0_first")
+        gate(gate0_first[:], w_block0, x_first, "0_first")
+        put(0, first, gate0_first[:])
+
         look_up(1)
-        wq1 = quantize(weave_w(1), P, "w1")
-        g0b = keep.tile([P, C], F32, name="gate0b", tag="w_raw1", align_bytes=64)
-        gate("0b", xqb, wq0, g0b[:])
-        g1 = keep.tile([P, S], F32, name="gate1")
-        gate("1a", xqa, wq1, g1[:, first])
-        gate("1b", xqb, wq1, g1[:, second])
-        put(0, second, g0b[:])
+        w_block1 = quantize_weights(1)
+        gate0_second = keep.tile([P, HALF], F32, name="gate0_second", tag="w_raw1", align_bytes=64)
+        gate(gate0_second[:], w_block0, x_second, "0_second")
+        gate1 = keep.tile([P, S], F32, name="gate1")
+        gate(gate1[:, first], w_block1, x_first, "1_first")
+        gate(gate1[:, second], w_block1, x_second, "1_second")
+        put(0, second, gate0_second[:])
         nc.sync.dma_start(out[0:P, :], store[0][:])
-        put(1, slice(0, S), g1[:])
+        put(1, whole, gate1[:])
         nc.sync.dma_start(out[P : 2 * P, :], store[1][:])

@@ -33,9 +33,7 @@ def tile_picked_idxput_gate_e_kernel(tc, xT, mem, w1, offs, slot, out):
         slot_sb = keep.tile([P, S // PER_COLUMN], U16, name="slot_sb")
         planes = [keep.tile([P, T], F32, name="plane%d" % t) for t in range(PACK)]
         store = [keep.tile([P, U], F32, name="store%d" % b) for b in range(BLOCKS)]
-        w_raw = [
-            keep.tile([P, PACK, P], F32, name="w_raw%d" % b, tag="w_raw%d" % b, align_bytes=64) for b in range(BLOCKS)
-        ]
+        w_raw = keep.tile([P, PACK, N], F32, name="w_raw", align_bytes=64)
 
         warm_in = keep.tile([P, 1], F32, name="warm_in")
         warm_out = keep.tile([P, 1], F32, name="warm_out")
@@ -43,49 +41,46 @@ def tile_picked_idxput_gate_e_kernel(tc, xT, mem, w1, offs, slot, out):
         nc.scalar.activation(warm_out[:], warm_in[:], SIGMOID)
 
         x_rows = xT.rearrange("(p t) c -> p t c", t=PACK)
-        w_rows = w1.rearrange("(p t) n -> p t n", t=PACK)
-        nc.sync.dma_start(planes[2][:], x_rows[:, 2, :])
+        nc.sync.dma_start(planes[0][:], x_rows[:, 0, :])
         nc.sync.dma_start(offs_sb[:], offs)
-        for t in (0, 1, 3):
+        for t in (1, 2, 3):
             nc.sync.dma_start(planes[t][:], x_rows[:, t, :])
-        nc.sync.dma_start(w_raw[0][:], w_rows[:, :, 0:P])
+        nc.sync.dma_start(w_raw[:], w1.rearrange("(p t) n -> p t n", t=PACK))
         nc.sync.dma_start(slot_sb[:], slot)
         nc.sync.dma_start(store[0][:], mem[0:P, :])
-        nc.sync.dma_start(w_raw[1][:], w_rows[:, :, P : 2 * P])
         nc.sync.dma_start(store[1][:], mem[P : 2 * P, :])
 
-        first, second, whole = slice(0, HALF), slice(HALF, S), slice(0, S)
+        first, second = slice(0, HALF), slice(HALF, S)
 
         def entries(list_sb, cols):
             return list_sb[:, cols.start // PER_COLUMN : cols.stop // PER_COLUMN]
 
-        def pick(dst, t, cols):
-            nc.vector.tensor_copy(dst, planes[t][:].indirect(entries(offs_sb, cols)))
+        def x_window(t, cols):
+            return planes[t][:].indirect(entries(offs_sb, cols))
 
-        def weave(dst, src):
-            nc.scalar.copy(
-                dst[:].rearrange("p (c i) t -> p c t i", i=RUN), src[:].rearrange("p t (c i) -> p c t i", i=RUN)
-            )
+        def mem_window(b, cols):
+            return store[b][:].indirect(entries(slot_sb, cols))
 
-        woven_first = keep.tile([P, HALF, PACK], BF16, name="woven_first", align_bytes=64)
+        x_woven = [keep.tile([P, HALF, PACK], BF16, name="x_woven%d" % h, align_bytes=64) for h in range(2)]
         picked_first = keep.tile([P, 2, HALF], BF16, name="picked_first", align_bytes=64)
-        picked_second = keep.tile([P, PACK, HALF], BF16, name="picked_second", align_bytes=64)
-        rounded = keep.tile([P, T], BF16, name="rounded", align_bytes=64)
-        pick(woven_first[:, :, 2], 2, first)
-        pick(picked_second[:, 2, :], 2, second)
-        pick(picked_first[:, 0, :], 0, first)
-        nc.scalar.copy(rounded[:], planes[0][:])
-        nc.scalar.activation(picked_second[:, 0, :], rounded[:].indirect(entries(offs_sb, second)), COPY)
-        pick(picked_first[:, 1, :], 1, first)
-        nc.scalar.copy(woven_first[:, :, 0:2], picked_first[:].rearrange("p t c -> p c t"))
-        pick(picked_second[:, 1, :], 1, second)
-        pick(woven_first[:, :, 3], 3, first)
-        pick(picked_second[:, 3, :], 3, second)
+        picked_second = [keep.tile([P, 2, HALF], BF16, name="picked_second%d" % u, align_bytes=64) for u in range(2)]
+        for t in range(2):
+            nc.vector.tensor_copy(picked_first[:, t, :], x_window(t, first))
+            nc.scalar.activation(picked_second[0][:, t, :], x_window(t, second), COPY)
+        nc.vector.tensor_copy(x_woven[0][:, :, 0:2], picked_first[:].rearrange("p t c -> p c t"))
+        nc.scalar.copy(x_woven[1][:, :, 0:2], picked_second[0][:].rearrange("p t c -> p c t"))
+        for t in range(2, 4):
+            nc.vector.tensor_copy(x_woven[0][:, :, t], x_window(t, first))
+            nc.scalar.activation(picked_second[1][:, t - 2, :], x_window(t, second), COPY)
+        nc.scalar.copy(x_woven[1][:, :, 2:4], picked_second[1][:].rearrange("p t c -> p c t"))
 
-        old = [keep.tile([P, S], F32, name="old%d" % b) for b in range(BLOCKS)]
+        w_woven = [keep.tile([P, P, PACK], BF16, name="w_woven%d" % b, align_bytes=64) for b in range(BLOCKS)]
 
-        def look_up(b):
-            nc.vector.tensor_copy(old[b][:], store[b][:].indirect(slot_sb[:]))
+        def weave(copy, b):
+            copy(
+                w_woven[b][:].rearrange("p (c i) t -> p c t i", i=RUN),
+                w_raw[:, :, b * P : (b + 1) * P].rearrange("p t (c i) -> p c t i", i=RUN),
+            )
 
         def quantize(woven, width, name):
             codes = keep.tile([P, width], U32, name=name + "_codes", align_bytes=64)
@@ -95,17 +90,18 @@ def tile_picked_idxput_gate_e_kernel(tc, xT, mem, w1, offs, slot, out):
             )
             return codes, scales
 
-        def quantize_weights(b):
-            woven = keep.tile([P, P, PACK], BF16, name="w_woven%d" % b, align_bytes=64)
-            weave(woven, w_raw[b])
-            return quantize(woven, P, "w%d" % b)
+        x_first = quantize(x_woven[0], HALF, "x_first")
+        weave(nc.vector.tensor_copy, 0)
+        weave(nc.scalar.copy, 1)
+        x_second = quantize(x_woven[1], HALF, "x_second")
+        w_mx = [quantize(w_woven[b], P, "w%d" % b) for b in range(BLOCKS)]
 
-        def gate(dst, w_mx, x_mx, name):
+        def gate(dst, b, x_mx, name):
             acc = psum.tile([P, HALF], F32, name="acc_" + name)
             nc.tensor.matmul_mx(
                 out=acc[:],
-                lhsT=w_mx[0][:].bitcast(FP8X4),
-                lhsT_scale=w_mx[1][:],
+                lhsT=w_mx[b][0][:].bitcast(FP8X4),
+                lhsT_scale=w_mx[b][1][:],
                 rhs=x_mx[0][:].bitcast(FP8X4),
                 rhs_scale=x_mx[1][:],
                 start=True,
@@ -113,27 +109,22 @@ def tile_picked_idxput_gate_e_kernel(tc, xT, mem, w1, offs, slot, out):
             )
             nc.scalar.activation(dst, acc[:], SIGMOID)
 
-        def put(b, cols, gates):
-            nc.vector.tensor_tensor(store[b][:].indirect(entries(slot_sb, cols)), old[b][:, cols], gates, MULT)
-
-        x_first = quantize(woven_first, HALF, "x_first")
-        w_block0 = quantize_weights(0)
-        look_up(0)
-        woven_second = keep.tile([P, HALF, PACK], BF16, name="woven_second", tag="w_raw0", align_bytes=64)
-        weave(woven_second, picked_second)
-        x_second = quantize(woven_second, HALF, "x_second")
-        gate0_first = keep.tile([P, HALF], F32, name="gate0_first")
-        gate(gate0_first[:], w_block0, x_first, "0_first")
-        put(0, first, gate0_first[:])
-
-        look_up(1)
-        w_block1 = quantize_weights(1)
-        gate0_second = keep.tile([P, HALF], F32, name="gate0_second", tag="w_raw1", align_bytes=64)
-        gate(gate0_second[:], w_block0, x_second, "0_second")
+        old0_second = keep.tile([P, HALF], F32, name="old0_second")
+        nc.vector.tensor_copy(old0_second[:], mem_window(0, second))
+        gate0_first = keep.tile([P, HALF], F32, name="gate0_first", tag="shared")
+        gate0_second = keep.tile([P, HALF], F32, name="gate0_second")
         gate1 = keep.tile([P, S], F32, name="gate1")
-        gate(gate1[:, first], w_block1, x_first, "1_first")
-        gate(gate1[:, second], w_block1, x_second, "1_second")
-        put(0, second, gate0_second[:])
+        gate(gate0_first[:], 0, x_first, "0_first")
+        gate(gate0_second[:], 0, x_second, "0_second")
+        gate(gate1[:, first], 1, x_first, "1_first")
+        gate(gate1[:, second], 1, x_second, "1_second")
+        new0 = [keep.tile([P, HALF], F32, name="new0_%d" % h) for h in range(2)]
+        nc.vector.tensor_tensor(new0[0][:], mem_window(0, first), gate0_first[:], MULT)
+        nc.vector.tensor_tensor(new0[1][:], old0_second[:], gate0_second[:], MULT)
+        nc.scalar.activation(mem_window(0, first), new0[0][:], COPY)
+        nc.scalar.activation(mem_window(0, second), new0[1][:], COPY)
         nc.sync.dma_start(out[0:P, :], store[0][:])
-        put(1, whole, gate1[:])
+        old1 = keep.tile([P, S], F32, name="old1", tag="shared")
+        nc.vector.tensor_copy(old1[:], store[1][:].indirect(slot_sb[:]))
+        nc.vector.tensor_tensor(store[1][:].indirect(slot_sb[:]), old1[:], gate1[:], MULT)
         nc.sync.dma_start(out[P : 2 * P, :], store[1][:])

@@ -21,6 +21,7 @@ HALF = S // 2
 BLOCKS = N // P
 PER_COLUMN = 16
 RUN = 4
+LEAD = 128
 
 
 def tile_picked_idxput_gate_e_kernel(tc, xT, mem, w1, offs, slot, out):
@@ -31,9 +32,9 @@ def tile_picked_idxput_gate_e_kernel(tc, xT, mem, w1, offs, slot, out):
 
         offs_sb = keep.tile([P, S // PER_COLUMN], U16, name="offs_sb")
         slot_sb = keep.tile([P, S // PER_COLUMN], U16, name="slot_sb")
-        planes = [keep.tile([P, T], F32, name="plane%d" % t) for t in range(PACK)]
+        planes = [keep.tile([P, T], F32, name="plane%d" % t, tag="plane%d" % t, align_bytes=64) for t in range(PACK)]
         store = [keep.tile([P, U], F32, name="store%d" % b) for b in range(BLOCKS)]
-        w_raw = keep.tile([P, PACK, N], F32, name="w_raw", align_bytes=64)
+        w_raw = [keep.tile([P, PACK, P], F32, name="w_raw%d" % b, tag="w_raw%d" % b, align_bytes=64) for b in range(BLOCKS)]
 
         warm_in = keep.tile([P, 1], F32, name="warm_in")
         warm_out = keep.tile([P, 1], F32, name="warm_out")
@@ -45,7 +46,9 @@ def tile_picked_idxput_gate_e_kernel(tc, xT, mem, w1, offs, slot, out):
         nc.sync.dma_start(offs_sb[:], offs)
         for t in (1, 2, 3):
             nc.sync.dma_start(planes[t][:], x_rows[:, t, :])
-        nc.sync.dma_start(w_raw[:], w1.rearrange("(p t) n -> p t n", t=PACK))
+        w_rows = w1.rearrange("(p t) n -> p t n", t=PACK)
+        for b in range(BLOCKS):
+            nc.sync.dma_start(w_raw[b][:], w_rows[:, :, b * P : (b + 1) * P])
         nc.sync.dma_start(slot_sb[:], slot)
         nc.sync.dma_start(store[0][:], mem[0:P, :])
         nc.sync.dma_start(store[1][:], mem[P : 2 * P, :])
@@ -62,39 +65,38 @@ def tile_picked_idxput_gate_e_kernel(tc, xT, mem, w1, offs, slot, out):
             return store[b][:].indirect(entries(slot_sb, cols))
 
         x_woven = [keep.tile([P, HALF, PACK], BF16, name="x_woven%d" % h, align_bytes=64) for h in range(2)]
-        picked_first = keep.tile([P, 2, HALF], BF16, name="picked_first", align_bytes=64)
         picked_second = [keep.tile([P, 2, HALF], BF16, name="picked_second%d" % u, align_bytes=64) for u in range(2)]
         for t in range(2):
-            nc.vector.tensor_copy(picked_first[:, t, :], x_window(t, first))
+            nc.vector.tensor_copy(x_woven[0][:, :, t], x_window(t, first))
             nc.scalar.activation(picked_second[0][:, t, :], x_window(t, second), COPY)
-        nc.vector.tensor_copy(x_woven[0][:, :, 0:2], picked_first[:].rearrange("p t c -> p c t"))
-        nc.scalar.copy(x_woven[1][:, :, 0:2], picked_second[0][:].rearrange("p t c -> p c t"))
+        nc.vector.tensor_copy(x_woven[1][:, :, 0:2], picked_second[0][:].rearrange("p t c -> p c t"))
         for t in range(2, 4):
             nc.vector.tensor_copy(x_woven[0][:, :, t], x_window(t, first))
             nc.scalar.activation(picked_second[1][:, t - 2, :], x_window(t, second), COPY)
-        nc.scalar.copy(x_woven[1][:, :, 2:4], picked_second[1][:].rearrange("p t c -> p c t"))
+        nc.vector.tensor_copy(x_woven[1][:, :, 2:4], picked_second[1][:].rearrange("p t c -> p c t"))
 
         w_woven = [keep.tile([P, P, PACK], BF16, name="w_woven%d" % b, align_bytes=64) for b in range(BLOCKS)]
 
         def weave(copy, b):
             copy(
                 w_woven[b][:].rearrange("p (c i) t -> p c t i", i=RUN),
-                w_raw[:, :, b * P : (b + 1) * P].rearrange("p t (c i) -> p c t i", i=RUN),
+                w_raw[b][:].rearrange("p t (c i) -> p c t i", i=RUN),
             )
 
-        def quantize(woven, width, name):
-            codes = keep.tile([P, width], U32, name=name + "_codes", align_bytes=64)
+        def quantize(woven, width, name, tag):
+            codes = keep.tile([P, width], U32, name=name + "_codes", tag=tag, align_bytes=64)
             scales = keep.tile([P, width], U8, name=name + "_scales", align_bytes=64)
             nc.vector.quantize_mx(
                 out=codes[:].bitcast(FP8X4), scales=scales[:], in_=woven[:].rearrange("p c t -> p (c t)")
             )
             return codes, scales
 
-        x_first = quantize(x_woven[0], HALF, "x_first")
-        weave(nc.vector.tensor_copy, 0)
+        weave(nc.scalar.copy, 0)
         weave(nc.scalar.copy, 1)
-        x_second = quantize(x_woven[1], HALF, "x_second")
-        w_mx = [quantize(w_woven[b], P, "w%d" % b) for b in range(BLOCKS)]
+        x_first = quantize(x_woven[0], HALF, "x_first", "plane3")
+        w_mx = [quantize(w_woven[0], P, "w0", "w0_codes")]
+        x_second = quantize(x_woven[1], HALF, "x_second", "w_raw0")
+        w_mx.append(quantize(w_woven[1], P, "w1", "w1_codes"))
 
         def gate(dst, b, x_mx, name):
             acc = psum.tile([P, HALF], F32, name="acc_" + name)
@@ -109,22 +111,22 @@ def tile_picked_idxput_gate_e_kernel(tc, xT, mem, w1, offs, slot, out):
             )
             nc.scalar.activation(dst, acc[:], SIGMOID)
 
-        old0_second = keep.tile([P, HALF], F32, name="old0_second")
-        nc.vector.tensor_copy(old0_second[:], mem_window(0, second))
-        gate0_first = keep.tile([P, HALF], F32, name="gate0_first", tag="shared")
-        gate0_second = keep.tile([P, HALF], F32, name="gate0_second")
+        lead, rest = slice(0, LEAD), slice(LEAD, S)
+        old0 = keep.tile([P, S], F32, name="old0")
+        gate0 = keep.tile([P, S], F32, name="gate0")
+        new0 = keep.tile([P, S], F32, name="new0")
         gate1 = keep.tile([P, S], F32, name="gate1")
-        gate(gate0_first[:], 0, x_first, "0_first")
-        gate(gate0_second[:], 0, x_second, "0_second")
+        old1 = keep.tile([P, S], F32, name="old1")
+        nc.vector.tensor_copy(old0[:, lead], mem_window(0, lead))
+        nc.vector.tensor_copy(old0[:, rest], mem_window(0, rest))
+        gate(gate0[:, first], 0, x_first, "0_first")
+        gate(gate0[:, second], 0, x_second, "0_second")
         gate(gate1[:, first], 1, x_first, "1_first")
         gate(gate1[:, second], 1, x_second, "1_second")
-        new0 = [keep.tile([P, HALF], F32, name="new0_%d" % h) for h in range(2)]
-        nc.vector.tensor_tensor(new0[0][:], mem_window(0, first), gate0_first[:], MULT)
-        nc.vector.tensor_tensor(new0[1][:], old0_second[:], gate0_second[:], MULT)
-        nc.scalar.activation(mem_window(0, first), new0[0][:], COPY)
-        nc.scalar.activation(mem_window(0, second), new0[1][:], COPY)
+        for cols in (lead, rest):
+            nc.gpsimd.tensor_tensor(new0[:, cols], old0[:, cols], gate0[:, cols], MULT)
+            nc.scalar.activation(mem_window(0, cols), new0[:, cols], COPY)
         nc.sync.dma_start(out[0:P, :], store[0][:])
-        old1 = keep.tile([P, S], F32, name="old1", tag="shared")
         nc.vector.tensor_copy(old1[:], store[1][:].indirect(slot_sb[:]))
         nc.vector.tensor_tensor(store[1][:].indirect(slot_sb[:]), old1[:], gate1[:], MULT)
         nc.sync.dma_start(out[P : 2 * P, :], store[1][:])

@@ -22,6 +22,7 @@ BLOCKS = N // P
 PER_COLUMN = 16
 RUN = 4
 LEAD = 128
+SPLIT = 256
 
 
 def tile_picked_idxput_gate_e_kernel(tc, xT, mem, w1, offs, slot, out):
@@ -47,10 +48,10 @@ def tile_picked_idxput_gate_e_kernel(tc, xT, mem, w1, offs, slot, out):
         for t in (1, 2, 3):
             nc.sync.dma_start(planes[t][:], x_rows[:, t, :])
         w_rows = w1.rearrange("(p t) n -> p t n", t=PACK)
-        for b in range(BLOCKS):
-            nc.sync.dma_start(w_raw[b][:], w_rows[:, :, b * P : (b + 1) * P])
         nc.sync.dma_start(slot_sb[:], slot)
+        nc.sync.dma_start(w_raw[0][:], w_rows[:, :, 0:P])
         nc.sync.dma_start(store[0][:], mem[0:P, :])
+        nc.sync.dma_start(w_raw[1][:], w_rows[:, :, P:N])
         nc.sync.dma_start(store[1][:], mem[P : 2 * P, :])
 
         first, second = slice(0, HALF), slice(HALF, S)
@@ -75,7 +76,7 @@ def tile_picked_idxput_gate_e_kernel(tc, xT, mem, w1, offs, slot, out):
             nc.scalar.activation(picked_second[1][:, t - 2, :], x_window(t, second), COPY)
         nc.vector.tensor_copy(x_woven[1][:, :, 2:4], picked_second[1][:].rearrange("p t c -> p c t"))
 
-        w_woven = [keep.tile([P, P, PACK], BF16, name="w_woven%d" % b, align_bytes=64) for b in range(BLOCKS)]
+        w_woven = [keep.tile([P, P, PACK], BF16, name="w_woven%d" % b, tag="w_woven%d" % b, align_bytes=64) for b in range(BLOCKS)]
 
         def weave(copy, b):
             copy(
@@ -92,11 +93,9 @@ def tile_picked_idxput_gate_e_kernel(tc, xT, mem, w1, offs, slot, out):
             return codes, scales
 
         weave(nc.scalar.copy, 0)
-        weave(nc.scalar.copy, 1)
         x_first = quantize(x_woven[0], HALF, "x_first", "plane3")
         w_mx = [quantize(w_woven[0], P, "w0", "w0_codes")]
         x_second = quantize(x_woven[1], HALF, "x_second", "w_raw0")
-        w_mx.append(quantize(w_woven[1], P, "w1", "w1_codes"))
 
         def gate(dst, b, x_mx, name):
             acc = psum.tile([P, HALF], F32, name="acc_" + name)
@@ -112,20 +111,26 @@ def tile_picked_idxput_gate_e_kernel(tc, xT, mem, w1, offs, slot, out):
             nc.scalar.activation(dst, acc[:], SIGMOID)
 
         lead, rest = slice(0, LEAD), slice(LEAD, S)
-        old0 = keep.tile([P, S], F32, name="old0")
+        old0_lead = keep.tile([P, LEAD], F32, name="old0_lead", tag="old0_lead")
+        old0_rest = keep.tile([P, S - LEAD], F32, name="old0_rest")
         gate0 = keep.tile([P, S], F32, name="gate0")
-        new0 = keep.tile([P, S], F32, name="new0")
-        gate1 = keep.tile([P, S], F32, name="gate1")
+        new0_lead = keep.tile([P, LEAD], F32, name="new0_lead")
         old1 = keep.tile([P, S], F32, name="old1")
-        nc.vector.tensor_copy(old0[:, lead], mem_window(0, lead))
-        nc.vector.tensor_copy(old0[:, rest], mem_window(0, rest))
+        nc.vector.tensor_copy(old0_lead[:], mem_window(0, lead))
+        nc.scalar.activation(old0_rest[:, SPLIT - LEAD :], mem_window(0, slice(SPLIT, S)), COPY)
+        nc.vector.tensor_copy(old0_rest[:, : SPLIT - LEAD], mem_window(0, slice(LEAD, SPLIT)))
+        weave(nc.vector.tensor_copy, 1)
         gate(gate0[:, first], 0, x_first, "0_first")
         gate(gate0[:, second], 0, x_second, "0_second")
+        nc.vector.tensor_tensor(new0_lead[:], old0_lead[:], gate0[:, lead], MULT)
+        nc.scalar.activation(mem_window(0, lead), new0_lead[:], COPY)
+        w_mx.append(quantize(w_woven[1], P, "w1", "w1_codes"))
+        gate1 = keep.tile([P, S], F32, name="gate1")
         gate(gate1[:, first], 1, x_first, "1_first")
         gate(gate1[:, second], 1, x_second, "1_second")
-        for cols in (lead, rest):
-            nc.gpsimd.tensor_tensor(new0[:, cols], old0[:, cols], gate0[:, cols], MULT)
-            nc.scalar.activation(mem_window(0, cols), new0[:, cols], COPY)
+        new0_rest = keep.tile([P, S - LEAD], F32, name="new0_rest", tag="w_woven1", align_bytes=64)
+        nc.gpsimd.tensor_tensor(new0_rest[:], old0_rest[:], gate0[:, rest], MULT)
+        nc.scalar.activation(mem_window(0, rest), new0_rest[:], COPY)
         nc.sync.dma_start(out[0:P, :], store[0][:])
         nc.vector.tensor_copy(old1[:], store[1][:].indirect(slot_sb[:]))
         nc.vector.tensor_tensor(store[1][:].indirect(slot_sb[:]), old1[:], gate1[:], MULT)

@@ -22,7 +22,7 @@ BLOCKS = N // P
 PER_COLUMN = 16
 RUN = 4
 LEAD = 128
-SPLIT = 256
+SPLIT = 384
 
 
 def tile_picked_idxput_gate_e_kernel(tc, xT, mem, w1, offs, slot, out):
@@ -31,28 +31,29 @@ def tile_picked_idxput_gate_e_kernel(tc, xT, mem, w1, offs, slot, out):
         keep = ctx.enter_context(tc.tile_pool(name="keep", bufs=1))
         psum = ctx.enter_context(tc.psum_pool(name="psum", bufs=1))
 
-        offs_sb = keep.tile([P, S // PER_COLUMN], U16, name="offs_sb")
-        slot_sb = keep.tile([P, S // PER_COLUMN], U16, name="slot_sb")
-        planes = [keep.tile([P, T], F32, name="plane%d" % t, tag="plane%d" % t, align_bytes=64) for t in range(PACK)]
-        store = [keep.tile([P, U], F32, name="store%d" % b) for b in range(BLOCKS)]
-        w_raw = [keep.tile([P, PACK, P], F32, name="w_raw%d" % b, tag="w_raw%d" % b, align_bytes=64) for b in range(BLOCKS)]
+        def sbuf(shape, dtype, name, tag=None):
+            return keep.tile(shape, dtype, name=name, tag=tag or name, align_bytes=64)
 
-        warm_in = keep.tile([P, 1], F32, name="warm_in")
-        warm_out = keep.tile([P, 1], F32, name="warm_out")
+        offs_sb = sbuf([P, S // PER_COLUMN], U16, "offs_sb")
+        slot_sb = sbuf([P, S // PER_COLUMN], U16, "slot_sb")
+        planes = [sbuf([P, T], F32, "plane%d" % t) for t in range(PACK)]
+        store = [sbuf([P, U], F32, "store%d" % b) for b in range(BLOCKS)]
+        w_raw = sbuf([P, PACK, N], F32, "w_raw")
+
+        warm_in = sbuf([P, 1], F32, "warm_in")
+        warm_out = sbuf([P, 1], F32, "warm_out")
         nc.vector.memset(warm_in[:], 0.0)
         nc.scalar.activation(warm_out[:], warm_in[:], SIGMOID)
 
         x_rows = xT.rearrange("(p t) c -> p t c", t=PACK)
         nc.sync.dma_start(planes[0][:], x_rows[:, 0, :])
         nc.sync.dma_start(offs_sb[:], offs)
-        for t in (1, 2, 3):
+        for t in range(1, PACK):
             nc.sync.dma_start(planes[t][:], x_rows[:, t, :])
-        w_rows = w1.rearrange("(p t) n -> p t n", t=PACK)
         nc.sync.dma_start(slot_sb[:], slot)
-        nc.sync.dma_start(w_raw[0][:], w_rows[:, :, 0:P])
-        nc.sync.dma_start(store[0][:], mem[0:P, :])
-        nc.sync.dma_start(w_raw[1][:], w_rows[:, :, P:N])
-        nc.sync.dma_start(store[1][:], mem[P : 2 * P, :])
+        nc.sync.dma_start(w_raw[:], w1.rearrange("(p t) n -> p t n", t=PACK))
+        for b in range(BLOCKS):
+            nc.sync.dma_start(store[b][:], mem[b * P : (b + 1) * P, :])
 
         first, second = slice(0, HALF), slice(HALF, S)
 
@@ -65,44 +66,36 @@ def tile_picked_idxput_gate_e_kernel(tc, xT, mem, w1, offs, slot, out):
         def mem_window(b, cols):
             return store[b][:].indirect(entries(slot_sb, cols))
 
-        x_woven = [keep.tile([P, HALF, PACK], BF16, name="x_woven%d" % h, align_bytes=64) for h in range(2)]
-        picked_second = [keep.tile([P, 2, HALF], BF16, name="picked_second%d" % u, align_bytes=64) for u in range(2)]
-        for t in range(2):
-            nc.vector.tensor_copy(x_woven[0][:, :, t], x_window(t, first))
-            nc.scalar.activation(picked_second[0][:, t, :], x_window(t, second), COPY)
-        nc.vector.tensor_copy(x_woven[1][:, :, 0:2], picked_second[0][:].rearrange("p t c -> p c t"))
-        for t in range(2, 4):
-            nc.vector.tensor_copy(x_woven[0][:, :, t], x_window(t, first))
-            nc.scalar.activation(picked_second[1][:, t - 2, :], x_window(t, second), COPY)
-        nc.vector.tensor_copy(x_woven[1][:, :, 2:4], picked_second[1][:].rearrange("p t c -> p c t"))
-
-        w_woven = [keep.tile([P, P, PACK], BF16, name="w_woven%d" % b, tag="w_woven%d" % b, align_bytes=64) for b in range(BLOCKS)]
+        x_woven = [sbuf([P, HALF, PACK], BF16, "x_woven%d" % h) for h in range(2)]
+        for u in range(2):
+            picked = sbuf([P, 2, HALF], BF16, "picked%d" % u)
+            for e in range(2):
+                nc.vector.tensor_copy(x_woven[0][:, :, 2 * u + e], x_window(2 * u + e, first))
+                nc.scalar.activation(picked[:, e, :], x_window(2 * u + e, second), COPY)
+            nc.vector.tensor_copy(x_woven[1][:, :, 2 * u : 2 * u + 2], picked[:].rearrange("p t c -> p c t"))
 
         def weave(copy, b):
+            woven = sbuf([P, P, PACK], BF16, "w_woven%d" % b)
             copy(
-                w_woven[b][:].rearrange("p (c i) t -> p c t i", i=RUN),
-                w_raw[b][:].rearrange("p t (c i) -> p c t i", i=RUN),
+                woven[:].rearrange("p (c i) t -> p c t i", i=RUN),
+                w_raw[:, :, b * P : (b + 1) * P].rearrange("p t (c i) -> p c t i", i=RUN),
             )
+            return woven
 
-        def quantize(woven, width, name, tag):
-            codes = keep.tile([P, width], U32, name=name + "_codes", tag=tag, align_bytes=64)
-            scales = keep.tile([P, width], U8, name=name + "_scales", align_bytes=64)
+        def quantize(woven, width, name, tag=None):
+            codes = sbuf([P, width], U32, name + "_codes", tag)
+            scales = sbuf([P, width], U8, name + "_scales")
             nc.vector.quantize_mx(
                 out=codes[:].bitcast(FP8X4), scales=scales[:], in_=woven[:].rearrange("p c t -> p (c t)")
             )
             return codes, scales
 
-        weave(nc.scalar.copy, 0)
-        x_first = quantize(x_woven[0], HALF, "x_first", "plane3")
-        w_mx = [quantize(w_woven[0], P, "w0", "w0_codes")]
-        x_second = quantize(x_woven[1], HALF, "x_second", "w_raw0")
-
-        def gate(dst, b, x_mx, name):
+        def gate(dst, w_mx, x_mx, name):
             acc = psum.tile([P, HALF], F32, name="acc_" + name)
             nc.tensor.matmul_mx(
                 out=acc[:],
-                lhsT=w_mx[b][0][:].bitcast(FP8X4),
-                lhsT_scale=w_mx[b][1][:],
+                lhsT=w_mx[0][:].bitcast(FP8X4),
+                lhsT_scale=w_mx[1][:],
                 rhs=x_mx[0][:].bitcast(FP8X4),
                 rhs_scale=x_mx[1][:],
                 start=True,
@@ -110,26 +103,33 @@ def tile_picked_idxput_gate_e_kernel(tc, xT, mem, w1, offs, slot, out):
             )
             nc.scalar.activation(dst, acc[:], SIGMOID)
 
+        w_woven0 = weave(nc.scalar.copy, 0)
+        x_first = quantize(x_woven[0], HALF, "x_first", "plane3")
+        x_second = quantize(x_woven[1], HALF, "x_second")
+        w_mx0 = quantize(w_woven0, P, "w0")
+        w_woven1 = weave(nc.scalar.copy, 1)
+
         lead, rest = slice(0, LEAD), slice(LEAD, S)
-        old0_lead = keep.tile([P, LEAD], F32, name="old0_lead", tag="old0_lead")
-        old0_rest = keep.tile([P, S - LEAD], F32, name="old0_rest")
-        gate0 = keep.tile([P, S], F32, name="gate0")
-        new0_lead = keep.tile([P, LEAD], F32, name="new0_lead")
-        old1 = keep.tile([P, S], F32, name="old1")
-        nc.vector.tensor_copy(old0_lead[:], mem_window(0, lead))
-        nc.scalar.activation(old0_rest[:, SPLIT - LEAD :], mem_window(0, slice(SPLIT, S)), COPY)
-        nc.vector.tensor_copy(old0_rest[:, : SPLIT - LEAD], mem_window(0, slice(LEAD, SPLIT)))
-        weave(nc.vector.tensor_copy, 1)
-        gate(gate0[:, first], 0, x_first, "0_first")
-        gate(gate0[:, second], 0, x_second, "0_second")
-        nc.vector.tensor_tensor(new0_lead[:], old0_lead[:], gate0[:, lead], MULT)
+        old0_tail = sbuf([P, S - SPLIT], F32, "old0_tail")
+        gate0 = sbuf([P, S], F32, "gate0")
+        gate1 = sbuf([P, S], F32, "gate1")
+        new0_lead = sbuf([P, LEAD], F32, "new0_lead")
+        old1 = sbuf([P, S], F32, "old1")
+        nc.scalar.activation(old0_tail[:], mem_window(0, slice(SPLIT, S)), COPY)
+        old0_lead = gate1[:, HALF : HALF + LEAD]
+        nc.vector.tensor_copy(old0_lead, mem_window(0, lead))
+        gate(gate0[:, first], w_mx0, x_first, "0_first")
+        gate(gate0[:, second], w_mx0, x_second, "0_second")
+        w_mx1 = quantize(w_woven1, P, "w1")
+        old0_mid = sbuf([P, SPLIT - LEAD], F32, "old0_mid", "w_raw")
+        nc.vector.tensor_copy(old0_mid[:], mem_window(0, slice(LEAD, SPLIT)))
+        gate(gate1[:, first], w_mx1, x_first, "1_first")
+        nc.vector.tensor_tensor(new0_lead[:], old0_lead, gate0[:, lead], MULT)
         nc.scalar.activation(mem_window(0, lead), new0_lead[:], COPY)
-        w_mx.append(quantize(w_woven[1], P, "w1", "w1_codes"))
-        gate1 = keep.tile([P, S], F32, name="gate1")
-        gate(gate1[:, first], 1, x_first, "1_first")
-        gate(gate1[:, second], 1, x_second, "1_second")
-        new0_rest = keep.tile([P, S - LEAD], F32, name="new0_rest", tag="w_woven1", align_bytes=64)
-        nc.gpsimd.tensor_tensor(new0_rest[:], old0_rest[:], gate0[:, rest], MULT)
+        gate(gate1[:, second], w_mx1, x_second, "1_second")
+        new0_rest = sbuf([P, S - LEAD], F32, "new0_rest", "w_woven1")
+        nc.gpsimd.tensor_tensor(new0_rest[:, SPLIT - LEAD :], old0_tail[:], gate0[:, SPLIT:], MULT)
+        nc.gpsimd.tensor_tensor(new0_rest[:, : SPLIT - LEAD], old0_mid[:], gate0[:, LEAD:SPLIT], MULT)
         nc.scalar.activation(mem_window(0, rest), new0_rest[:], COPY)
         nc.sync.dma_start(out[0:P, :], store[0][:])
         nc.vector.tensor_copy(old1[:], store[1][:].indirect(slot_sb[:]))

@@ -22,7 +22,9 @@ BLOCKS = N // P
 PER_COLUMN = 16
 RUN = 4
 LEAD = 128
-SPLIT = 384
+ALIGN = 256
+SHARE = 64
+SPLIT = 192
 
 
 def tile_picked_idxput_gate_e_kernel(tc, xT, mem, w1, offs, slot, out):
@@ -32,7 +34,7 @@ def tile_picked_idxput_gate_e_kernel(tc, xT, mem, w1, offs, slot, out):
         psum = ctx.enter_context(tc.psum_pool(name="psum", bufs=1))
 
         def sbuf(shape, dtype, name, tag=None):
-            return keep.tile(shape, dtype, name=name, tag=tag or name, align_bytes=64)
+            return keep.tile(shape, dtype, name=name, tag=tag or name, align_bytes=ALIGN)
 
         offs_sb = sbuf([P, S // PER_COLUMN], U16, "offs_sb")
         slot_sb = sbuf([P, S // PER_COLUMN], U16, "slot_sb")
@@ -67,69 +69,72 @@ def tile_picked_idxput_gate_e_kernel(tc, xT, mem, w1, offs, slot, out):
             return store[b][:].indirect(entries(slot_sb, cols))
 
         x_woven = [sbuf([P, HALF, PACK], BF16, "x_woven%d" % h) for h in range(2)]
-        for u in range(2):
-            picked = sbuf([P, 2, HALF], BF16, "picked%d" % u)
-            for e in range(2):
-                nc.vector.tensor_copy(x_woven[0][:, :, 2 * u + e], x_window(2 * u + e, first))
-                nc.scalar.activation(picked[:, e, :], x_window(2 * u + e, second), COPY)
-            nc.vector.tensor_copy(x_woven[1][:, :, 2 * u : 2 * u + 2], picked[:].rearrange("p t c -> p c t"))
+        for t in range(PACK):
+            nc.scalar.activation(x_woven[0][:, :, t], x_window(t, first), COPY)
+            nc.vector.tensor_copy(x_woven[1][:, :, t], x_window(t, second))
 
-        def weave(copy, b):
-            woven = sbuf([P, P, PACK], BF16, "w_woven%d" % b)
+        w_woven = [sbuf([P, P, PACK], BF16, "w_woven%d" % b) for b in range(BLOCKS)]
+
+        def weave(copy, b, lo, hi):
             copy(
-                woven[:].rearrange("p (c i) t -> p c t i", i=RUN),
-                w_raw[:, :, b * P : (b + 1) * P].rearrange("p t (c i) -> p c t i", i=RUN),
+                w_woven[b][:, lo:hi, :].rearrange("p (c i) t -> p c t i", i=RUN),
+                w_raw[:, :, b * P + lo : b * P + hi].rearrange("p t (c i) -> p c t i", i=RUN),
             )
-            return woven
 
-        def quantize(woven, width, name, tag=None):
-            codes = sbuf([P, width], U32, name + "_codes", tag)
-            scales = sbuf([P, width], U8, name + "_scales")
+        def mx_tiles(width, name, tag=None):
+            return sbuf([P, width], U32, name + "_codes", tag), sbuf([P, width], U8, name + "_scales")
+
+        def quantize(mx, cols, woven):
             nc.vector.quantize_mx(
-                out=codes[:].bitcast(FP8X4), scales=scales[:], in_=woven[:].rearrange("p c t -> p (c t)")
+                out=mx[0][:, cols].bitcast(FP8X4), scales=mx[1][:, cols], in_=woven[:].rearrange("p c t -> p (c t)")
             )
-            return codes, scales
 
-        def gate(dst, w_mx, x_mx, name):
-            acc = psum.tile([P, HALF], F32, name="acc_" + name)
+        def project(acc, w_mx, cols):
             nc.tensor.matmul_mx(
-                out=acc[:],
+                out=acc,
                 lhsT=w_mx[0][:].bitcast(FP8X4),
                 lhsT_scale=w_mx[1][:],
-                rhs=x_mx[0][:].bitcast(FP8X4),
-                rhs_scale=x_mx[1][:],
+                rhs=x_mx[0][:, cols].bitcast(FP8X4),
+                rhs_scale=x_mx[1][:, cols],
                 start=True,
                 stop=True,
             )
-            nc.scalar.activation(dst, acc[:], SIGMOID)
 
-        w_woven0 = weave(nc.scalar.copy, 0)
-        x_first = quantize(x_woven[0], HALF, "x_first", "plane3")
-        x_second = quantize(x_woven[1], HALF, "x_second")
-        w_mx0 = quantize(w_woven0, P, "w0")
-        w_woven1 = weave(nc.scalar.copy, 1)
+        x_mx = mx_tiles(S, "x", "plane3")
+        quantize(x_mx, first, x_woven[0])
+        quantize(x_mx, second, x_woven[1])
+        weave(nc.scalar.copy, 0, 0, P)
+        weave(nc.vector.tensor_copy, 1, 0, SHARE)
+        weave(nc.scalar.copy, 1, SHARE, P)
+        w_mx = [mx_tiles(P, "w%d" % b) for b in range(BLOCKS)]
+        for b in range(BLOCKS):
+            quantize(w_mx[b], slice(0, P), w_woven[b])
 
         lead, rest = slice(0, LEAD), slice(LEAD, S)
-        old0_tail = sbuf([P, S - SPLIT], F32, "old0_tail")
-        gate0 = sbuf([P, S], F32, "gate0")
+        old0 = sbuf([P, S], F32, "old0")
         gate1 = sbuf([P, S], F32, "gate1")
+        gate0_lead = gate1[:, HALF : HALF + LEAD]
+        gate0_rest = sbuf([P, S - LEAD], F32, "gate0_rest")
         new0_lead = sbuf([P, LEAD], F32, "new0_lead")
+        new0_rest = sbuf([P, S - LEAD], F32, "new0_rest")
         old1 = sbuf([P, S], F32, "old1")
-        nc.scalar.activation(old0_tail[:], mem_window(0, slice(SPLIT, S)), COPY)
-        old0_lead = gate1[:, HALF : HALF + LEAD]
-        nc.vector.tensor_copy(old0_lead, mem_window(0, lead))
-        gate(gate0[:, first], w_mx0, x_first, "0_first")
-        gate(gate0[:, second], w_mx0, x_second, "0_second")
-        w_mx1 = quantize(w_woven1, P, "w1")
-        old0_mid = sbuf([P, SPLIT - LEAD], F32, "old0_mid", "w_raw")
-        nc.vector.tensor_copy(old0_mid[:], mem_window(0, slice(LEAD, SPLIT)))
-        gate(gate1[:, first], w_mx1, x_first, "1_first")
-        nc.vector.tensor_tensor(new0_lead[:], old0_lead, gate0[:, lead], MULT)
+        nc.scalar.activation(old0[:, :SPLIT], mem_window(0, slice(0, SPLIT)), COPY)
+        nc.vector.tensor_copy(old0[:, SPLIT:], mem_window(0, slice(SPLIT, S)))
+        acc_first = psum.tile([P, HALF], F32, name="acc_first")
+        acc_second = psum.tile([P, HALF], F32, name="acc_second")
+        acc1 = [psum.tile([P, HALF], F32, name="acc1_%d" % h) for h in range(2)]
+        project(acc_first[:], w_mx[0], first)
+        nc.scalar.activation(gate0_lead, acc_first[:, lead], SIGMOID)
+        nc.scalar.activation(gate0_rest[:, : HALF - LEAD], acc_first[:, LEAD:], SIGMOID)
+        project(acc_second[:], w_mx[0], second)
+        nc.scalar.activation(gate0_rest[:, HALF - LEAD :], acc_second[:], SIGMOID)
+        project(acc1[0][:], w_mx[1], first)
+        nc.scalar.activation(gate1[:, first], acc1[0][:], SIGMOID)
+        nc.vector.tensor_tensor(new0_lead[:], old0[:, lead], gate0_lead, MULT)
         nc.scalar.activation(mem_window(0, lead), new0_lead[:], COPY)
-        gate(gate1[:, second], w_mx1, x_second, "1_second")
-        new0_rest = sbuf([P, S - LEAD], F32, "new0_rest", "w_woven1")
-        nc.gpsimd.tensor_tensor(new0_rest[:, SPLIT - LEAD :], old0_tail[:], gate0[:, SPLIT:], MULT)
-        nc.gpsimd.tensor_tensor(new0_rest[:, : SPLIT - LEAD], old0_mid[:], gate0[:, LEAD:SPLIT], MULT)
+        project(acc1[1][:], w_mx[1], second)
+        nc.scalar.activation(gate1[:, second], acc1[1][:], SIGMOID)
+        nc.gpsimd.tensor_tensor(new0_rest[:], old0[:, rest], gate0_rest[:], MULT)
         nc.scalar.activation(mem_window(0, rest), new0_rest[:], COPY)
         nc.sync.dma_start(out[0:P, :], store[0][:])
         nc.vector.tensor_copy(old1[:], store[1][:].indirect(slot_sb[:]))

@@ -23,8 +23,8 @@ PER_COLUMN = 16
 RUN = 4
 LEAD = 128
 ALIGN = 256
-SHARE = 64
-SPLIT = 192
+SHARE = 32
+SPLIT = 224
 
 
 def tile_picked_idxput_gate_e_kernel(tc, xT, mem, w1, offs, slot, out):

@@ -40,7 +40,8 @@ def tile_picked_idxput_gate_e_kernel(tc, xT, mem, w1, offs, slot, out):
         slot_sb = sbuf([P, S // PER_COLUMN], U16, "slot_sb")
         planes = [sbuf([P, T], F32, "plane%d" % t) for t in range(PACK)]
         store = [sbuf([P, U], F32, "store%d" % b) for b in range(BLOCKS)]
-        w_raw = sbuf([P, PACK, N], F32, "w_raw")
+        w_rows = sbuf([P, PACK * N], F32, "w_raw")
+        w_raw = w_rows[:].rearrange("p (t n) -> p t n", t=PACK)
 
         warm_in = sbuf([P, 1], F32, "warm_in")
         warm_out = sbuf([P, 1], F32, "warm_out")
@@ -53,7 +54,7 @@ def tile_picked_idxput_gate_e_kernel(tc, xT, mem, w1, offs, slot, out):
         for t in range(1, PACK):
             nc.sync.dma_start(planes[t][:], x_rows[:, t, :])
         nc.sync.dma_start(slot_sb[:], slot)
-        nc.sync.dma_start(w_raw[:], w1.rearrange("(p t) n -> p t n", t=PACK))
+        nc.sync.dma_start(w_rows[:], w1.rearrange("(p t) n -> p (t n)", t=PACK))
         for b in range(BLOCKS):
             nc.sync.dma_start(store[b][:], mem[b * P : (b + 1) * P, :])
 
@@ -94,15 +95,15 @@ def tile_picked_idxput_gate_e_kernel(tc, xT, mem, w1, offs, slot, out):
                 out=acc,
                 lhsT=w_mx[0][:].bitcast(FP8X4),
                 lhsT_scale=w_mx[1][:],
-                rhs=x_mx[0][:, cols].bitcast(FP8X4),
-                rhs_scale=x_mx[1][:, cols],
+                rhs=x_mx[cols.start][0][:].bitcast(FP8X4),
+                rhs_scale=x_mx[cols.start][1][:],
                 start=True,
                 stop=True,
             )
 
-        x_mx = mx_tiles(S, "x", "plane3")
-        quantize(x_mx, first, x_woven[0])
-        quantize(x_mx, second, x_woven[1])
+        x_mx = {0: mx_tiles(HALF, "x_first"), HALF: mx_tiles(HALF, "x_second", "plane3")}
+        quantize(x_mx[0], first, x_woven[0])
+        quantize(x_mx[HALF], first, x_woven[1])
         weave(nc.scalar.copy, 0, 0, P)
         weave(nc.vector.tensor_copy, 1, 0, SHARE)
         weave(nc.scalar.copy, 1, SHARE, P)

@@ -55,8 +55,10 @@ def tile_picked_idxput_gate_e_kernel(tc, xT, mem, w1, offs, slot, out):
             nc.sync.dma_start(planes[t][:], x_rows[:, t, :])
         nc.sync.dma_start(slot_sb[:], slot)
         nc.sync.dma_start(w_rows[:], w1.rearrange("(p t) n -> p (t n)", t=PACK))
-        for b in range(BLOCKS):
-            nc.sync.dma_start(store[b][:], mem[b * P : (b + 1) * P, :])
+        source1 = sbuf([P, U], F32, "source1")
+        nc.sync.dma_start(store[0][:], mem[0:P, :])
+        nc.sync.dma_start(source1[:], mem[P : 2 * P, :])
+        nc.sync.dma_start(store[1][:], mem[P : 2 * P, :])
 
         first, second = slice(0, HALF), slice(HALF, S)
 
@@ -138,6 +140,8 @@ def tile_picked_idxput_gate_e_kernel(tc, xT, mem, w1, offs, slot, out):
         nc.gpsimd.tensor_tensor(new0_rest[:], old0[:, rest], gate0_rest[:], MULT)
         nc.scalar.activation(mem_window(0, rest), new0_rest[:], COPY)
         nc.sync.dma_start(out[0:P, :], store[0][:])
-        nc.vector.tensor_copy(old1[:], store[1][:].indirect(slot_sb[:]))
-        nc.vector.tensor_tensor(store[1][:].indirect(slot_sb[:]), old1[:], gate1[:], MULT)
+        for cols in (first, second):
+            nc.vector.tensor_copy(old1[:, cols], source1[:].indirect(entries(slot_sb, cols)))
+        for cols in (first, second):
+            nc.vector.tensor_tensor(mem_window(1, cols), old1[:, cols], gate1[:, cols], MULT)
         nc.sync.dma_start(out[P : 2 * P, :], store[1][:])

from contextlib import ExitStack

import concourse.mybir as mybir

K, T, S, N, U = 512, 1024, 512, 256, 1024
FLOPS = 2 * K * N * S

F32 = mybir.dt.float32
BF16 = mybir.dt.bfloat16
U32 = mybir.dt.uint32
U16 = mybir.dt.uint16
U8 = mybir.dt.uint8
FP8X4 = mybir.dt.float8_e4m3fn_x4
SIGMOID = mybir.ActivationFunctionType.Sigmoid
COPY = mybir.ActivationFunctionType.Copy
MULT = mybir.AluOpType.mult

P = 128
PACK = 4
HALF = S // 2
BLOCKS = N // P
PER_COLUMN = 16
RUN = 4
LEAD = 128
ALIGN = 256
SHARE = 32
SPLIT = 224


def tile_picked_idxput_gate_e_kernel(tc, xT, mem, w1, offs, slot, out):
    nc = tc.nc
    with ExitStack() as ctx:
        keep = ctx.enter_context(tc.tile_pool(name="keep", bufs=1))
        psum = ctx.enter_context(tc.psum_pool(name="psum", bufs=1))

        def sbuf(shape, dtype, name, tag=None):
            return keep.tile(shape, dtype, name=name, tag=tag or name, align_bytes=ALIGN)

        offs_sb = sbuf([P, S // PER_COLUMN], U16, "offs_sb")
        slot_sb = sbuf([P, S // PER_COLUMN], U16, "slot_sb")
        planes = [sbuf([P, T], F32, "plane%d" % t) for t in range(PACK)]
        store = [sbuf([P, U], F32, "store%d" % b) for b in range(BLOCKS)]
        w_rows = sbuf([P, PACK * N], F32, "w_raw")
        w_raw = w_rows[:].rearrange("p (t n) -> p t n", t=PACK)

        warm_in = sbuf([P, 1], F32, "warm_in")
        warm_out = sbuf([P, 1], F32, "warm_out")
        nc.vector.memset(warm_in[:], 0.0)
        nc.scalar.activation(warm_out[:], warm_in[:], SIGMOID)

        x_rows = xT.rearrange("(p t) c -> p t c", t=PACK)
        nc.sync.dma_start(planes[0][:], x_rows[:, 0, :])
        nc.sync.dma_start(offs_sb[:], offs)
        for t in range(1, PACK):
            nc.sync.dma_start(planes[t][:], x_rows[:, t, :])
        nc.sync.dma_start(slot_sb[:], slot)
        nc.sync.dma_start(w_rows[:], w1.rearrange("(p t) n -> p (t n)", t=PACK))
        source1 = sbuf([P, U], F32, "source1")
        nc.sync.dma_start(store[0][:], mem[0:P, :])
        nc.sync.dma_start(source1[:], mem[P : 2 * P, :])
        nc.sync.dma_start(store[1][:], mem[P : 2 * P, :])

        first, second = slice(0, HALF), slice(HALF, S)

        def entries(list_sb, cols):
            return list_sb[:, cols.start // PER_COLUMN : cols.stop // PER_COLUMN]

        def x_window(t, cols):
            return planes[t][:].indirect(entries(offs_sb, cols))

        def mem_window(b, cols):
            return store[b][:].indirect(entries(slot_sb, cols))

        x_woven = [sbuf([P, HALF, PACK], BF16, "x_woven%d" % h) for h in range(2)]
        for t in range(PACK):
            nc.scalar.activation(x_woven[0][:, :, t], x_window(t, first), COPY)
            nc.vector.tensor_copy(x_woven[1][:, :, t], x_window(t, second))

        w_woven = [sbuf([P, P, PACK], BF16, "w_woven%d" % b) for b in range(BLOCKS)]

        def weave(copy, b, lo, hi):
            copy(
                w_woven[b][:, lo:hi, :].rearrange("p (c i) t -> p c t i", i=RUN),
                w_raw[:, :, b * P + lo : b * P + hi].rearrange("p t (c i) -> p c t i", i=RUN),
            )

        def mx_tiles(width, name, tag=None):
            return sbuf([P, width], U32, name + "_codes", tag), sbuf([P, width], U8, name + "_scales")

        def quantize(mx, cols, woven):
            nc.vector.quantize_mx(
                out=mx[0][:, cols].bitcast(FP8X4), scales=mx[1][:, cols], in_=woven[:].rearrange("p c t -> p (c t)")
            )

        def project(acc, w_mx, cols):
            nc.tensor.matmul_mx(
                out=acc,
                lhsT=w_mx[0][:].bitcast(FP8X4),
                lhsT_scale=w_mx[1][:],
                rhs=x_mx[cols.start][0][:].bitcast(FP8X4),
                rhs_scale=x_mx[cols.start][1][:],
                start=True,
                stop=True,
            )

        x_mx = {0: mx_tiles(HALF, "x_first"), HALF: mx_tiles(HALF, "x_second", "plane3")}
        quantize(x_mx[0], first, x_woven[0])
        quantize(x_mx[HALF], first, x_woven[1])
        weave(nc.scalar.copy, 0, 0, P)
        weave(nc.vector.tensor_copy, 1, 0, SHARE)
        weave(nc.scalar.copy, 1, SHARE, P)
        w_mx = [mx_tiles(P, "w%d" % b) for b in range(BLOCKS)]
        for b in range(BLOCKS):
            quantize(w_mx[b], slice(0, P), w_woven[b])

        lead, rest = slice(0, LEAD), slice(LEAD, S)
        old0 = sbuf([P, S], F32, "old0")
        gate1 = sbuf([P, S], F32, "gate1")
        gate0_lead = gate1[:, HALF : HALF + LEAD]
        gate0_rest = sbuf([P, S - LEAD], F32, "gate0_rest")
        new0_lead = sbuf([P, LEAD], F32, "new0_lead")
        new0_rest = sbuf([P, S - LEAD], F32, "new0_rest")
        old1 = sbuf([P, S], F32, "old1")
        nc.scalar.activation(old0[:, :SPLIT], mem_window(0, slice(0, SPLIT)), COPY)
        nc.vector.tensor_copy(old0[:, SPLIT:], mem_window(0, slice(SPLIT, S)))
        acc_first = psum.tile([P, HALF], F32, name="acc_first")
        acc_second = psum.tile([P, HALF], F32, name="acc_second")
        acc1 = [psum.tile([P, HALF], F32, name="acc1_%d" % h) for h in range(2)]
        project(acc_first[:], w_mx[0], first)
        nc.scalar.activation(gate0_lead, acc_first[:, lead], SIGMOID)
        nc.scalar.activation(gate0_rest[:, : HALF - LEAD], acc_first[:, LEAD:], SIGMOID)
        project(acc_second[:], w_mx[0], second)
        nc.scalar.activation(gate0_rest[:, HALF - LEAD :], acc_second[:], SIGMOID)
        project(acc1[0][:], w_mx[1], first)
        nc.scalar.activation(gate1[:, first], acc1[0][:], SIGMOID)
        nc.vector.tensor_tensor(new0_lead[:], old0[:, lead], gate0_lead, MULT)
        nc.scalar.activation(mem_window(0, lead), new0_lead[:], COPY)
        project(acc1[1][:], w_mx[1], second)
        nc.scalar.activation(gate1[:, second], acc1[1][:], SIGMOID)
        nc.gpsimd.tensor_tensor(new0_rest[:], old0[:, rest], gate0_rest[:], MULT)
        nc.scalar.activation(mem_window(0, rest), new0_rest[:], COPY)
        nc.sync.dma_start(out[0:P, :], store[0][:])
        for cols in (first, second):
            nc.vector.tensor_copy(old1[:, cols], source1[:].indirect(entries(slot_sb, cols)))
        for cols in (first, second):
            nc.vector.tensor_tensor(mem_window(1, cols), old1[:, cols], gate1[:, cols], MULT)
        nc.sync.dma_start(out[P : 2 * P, :], store[1][:])
